import numpy as np
import ml_dtypes


def mxq(x, axis, fmt="e4m3"):
    dtype, down = {"e4m3": (ml_dtypes.float8_e4m3fn, 7), "e5m2": (ml_dtypes.float8_e5m2, 14)}[fmt]
    v = np.moveaxis(np.asarray(x, np.float32).astype(ml_dtypes.bfloat16).astype(np.float64), axis, -1)
    blocks = v.reshape(v.shape[:-1] + (-1, 32))
    amax = np.abs(blocks).max(-1, keepdims=True)
    byte = np.maximum(np.where(amax > 0, np.frexp(amax)[1] - 1 + 127, 0) - down, 1)
    scale = np.exp2(byte - 127.0)
    codes = (blocks / scale).astype(np.float32).astype(dtype).astype(np.float64)
    return np.moveaxis((codes * scale).reshape(v.shape), -1, axis)


WIDE = False


def mx_kscale(k):
    if not WIDE:
        return np.ones(k)
    levels = np.array([10, -10, 5, -5, 0])
    if k % 512:
        return np.exp2(np.random.permutation(np.resize(levels, k // 32))).repeat(32)
    a = np.empty((k // 512, 16))
    for p in range(k // 512):
        a[p, :8] = np.random.permutation(np.resize(levels, 8))
        for g in range(8):
            far = levels[np.abs(levels - a[p, g]) >= 10]
            a[p, g + 8] = far[np.random.randint(len(far))]
    return np.exp2(a.ravel()).repeat(32)


def f64(x):
    return np.asarray(x).astype(np.float64)


def striped(idx):
    return np.tile(np.asarray(idx).reshape(-1, 16).T, (8, 1)).astype(np.uint16)


def unstriped(offs):
    return offs[:16].T.reshape(-1).astype(np.int64)


B, N, T, D, DV, NQ = 4, 256, 2048, 1536, 0, 128


def setup_inputs():
    n = np.random.standard_normal
    seg = T // B
    idx = np.concatenate([b * seg + np.random.permutation(seg)[:N] for b in range(B)])
    s = mx_kscale(D)[:, None]
    return {
        "qT": (n((B, D, NQ)) * s * (1.00 / np.sqrt(D))).astype(np.float32),
        "kT": (n((D, T)) / s).astype(np.float32),
        "offs": striped(idx),
    }


def reference(qT, kT, offs):
    idx = unstriped(offs)
    pick = lambda x: x[:, idx].reshape(x.shape[0], B, N).transpose(1, 0, 2)
    a = mxq(f64(qT), 1, "e4m3").transpose(0, 2, 1) @ mxq(pick(f64(kT)), 1, "e4m3")
    out = np.zeros((B, NQ, T))
    for b in range(B):
        out[b][:, idx[b * N:(b + 1) * N]] = a[b]
    return out

@@ -1,0 +1,189 @@
+from contextlib import ExitStack
+
+import concourse.mybir as mybir
+
+FLOPS = 2 * 4 * 128 * 256 * 1536
+
+F32 = mybir.dt.float32
+BF16 = mybir.dt.bfloat16
+U32 = mybir.dt.uint32
+U16 = mybir.dt.uint16
+U8 = mybir.dt.uint8
+FP8X4 = mybir.dt.float8_e4m3fn_x4
+COPY = mybir.ActivationFunctionType.Copy
+MULT = mybir.AluOpType.mult
+ADD = mybir.AluOpType.add
+
+P = 128
+B = 4
+N = 256
+T = 2048
+SEG = T // B
+D = 1536
+M = 128
+K_PASS = 512
+G = D // K_PASS
+LOOKAHEAD = 9
+
+
+def tile_attend_sddmm_seg_kernel(tc, qT, kT, offs, out):
+    nc = tc.nc
+    units = [(b, g) for b in range(B) for g in range(G)]
+    last = len(units) - 1
+
+    with ExitStack() as ctx:
+        keep = ctx.enter_context(tc.tile_pool(name="keep", bufs=1))
+        raws = ctx.enter_context(tc.tile_pool(name="raws", bufs=LOOKAHEAD + 1))
+        ring = ctx.enter_context(tc.tile_pool(name="ring", bufs=4))
+        psum = ctx.enter_context(tc.psum_pool(name="psum", bufs=B))
+
+        offs_sb = keep.tile([P, B * N // 16], U16, name="offs_sb")
+        raw_k = {}
+        raw_q = {}
+
+        def load_k(i, pieces):
+            b, g = units[i]
+            rows = kT[g * K_PASS : (g + 1) * K_PASS, :].rearrange("(p t) c -> p t c", t=4)
+            raw = raws.tile([P, 4, SEG], F32, name="raw")
+            step = 4 // pieces
+            for t in range(0, 4, step):
+                nc.sync.dma_start(out=raw[:, t : t + step, :], in_=rows[:, t : t + step, b * SEG : (b + 1) * SEG])
+            raw_k[i] = raw
+
+        def load_q(b):
+            rq = keep.tile([P, G, 4 * M], F32, name=f"raw_q{b}")
+            nc.sync.dma_start(out=rq[:], in_=qT[b].rearrange("(g p t) m -> p g (t m)", p=P, t=4))
+            raw_q[b] = rq
+
+        load_k(0, 2)
+        nc.sync.dma_start(offs_sb[:], offs)
+        load_q(0)
+        for i in range(1, LOOKAHEAD):
+            load_k(i, 1)
+            if i % G == 0:
+                load_q(i // G)
+
+        zeros = keep.tile([P, T - SEG], F32, name="zeros")
+        placed = []
+        for b in range(B):
+            row = keep.tile([P, (b + 1) * SEG], F32, name=f"placed{b}")
+            placed.append(row)
+        for b in range(B):
+            nc.vector.memset(placed[b][:, b * SEG :], 0.0)
+        nc.vector.memset(zeros[:], 0.0)
+
+        pairs = []
+        for g in range(G):
+            pair = keep.tile([P, 2, T, 2], BF16, name=f"pairs{g}")
+            pairs.append(pair)
+
+        q_codes = []
+        q_scales = []
+        for b in range(B):
+            qc = keep.tile([P, G * M], U32, name=f"q_codes{b}", align_bytes=64)
+            qs = keep.tile([P, G * M], U8, name=f"q_scales{b}", align_bytes=64)
+            q_codes.append(qc)
+            q_scales.append(qs)
+
+        grouped_q = {}
+
+        def group_q(b):
+            gq = keep.tile([P, G * M * 4], BF16, name=f"grouped_q{b}", align_bytes=64)
+            nc.gpsimd.tensor_scalar(
+                out=gq[:].rearrange("p (g m t) -> p g m t", g=G, t=4),
+                in0=raw_q[b][:].rearrange("p g (t m) -> p g m t", t=4),
+                scalar1=1.0,
+                scalar2=0.0,
+                op0=MULT,
+                op1=ADD,
+            )
+            grouped_q[b] = gq
+
+        def quantize_q(b):
+            for lo, hi in ((0, 256), (256, 384)):
+                nc.vector.quantize_mx(
+                    out=q_codes[b][:, lo:hi].bitcast(FP8X4),
+                    scales=q_scales[b][:, lo:hi],
+                    in_=grouped_q[b][:, 4 * lo : 4 * hi],
+                )
+
+        def cast_k(i):
+            b, g = units[i]
+            cols = slice(b * SEG, (b + 1) * SEG)
+            src = raw_k[i][:].rearrange("p (u e) c -> p u c e", e=2)
+            if i in (0, last):
+                nc.scalar.activation(pairs[g][:, 0, cols, :], src[:, 0, :, :], COPY)
+                nc.vector.tensor_copy(pairs[g][:, 1, cols, :], src[:, 1, :, :])
+            else:
+                nc.scalar.activation(pairs[g][:, :, cols, :], src, COPY)
+
+        grouped_k = {}
+        codes_k = {}
+
+        def gather_k(i):
+            b, g = units[i]
+            gk = ring.tile([P, 4 * N], BF16, name="gk", align_bytes=64)
+            words = gk[:].bitcast(U32).rearrange("p (c u) -> p c u", u=2)
+            table = pairs[g][:].rearrange("p u c e -> p (u c e)").bitcast(U32)
+            for u in range(2):
+                nc.vector.tensor_copy(
+                    words[:, :, u],
+                    table[:, u * T : u * T + (b + 1) * SEG].indirect(offs_sb[:, b * (N // 16) : (b + 1) * (N // 16)]),
+                )
+            grouped_k[i] = gk
+
+        def quantize_k(i):
+            kc = ring.tile([P, N], U32, name="kc", align_bytes=64)
+            ks = ring.tile([P, N], U8, name="ks", align_bytes=64)
+            nc.vector.quantize_mx(out=kc[:].bitcast(FP8X4), scales=ks[:], in_=grouped_k[i][:])
+            codes_k[i] = (kc, ks)
+
+        banks = {}
+
+        def multiply(i):
+            b, g = units[i]
+            if g == 0:
+                acc = psum.tile([M, N], F32, name="acc")
+                banks[b] = acc
+            kc, ks = codes_k[i]
+            nc.tensor.matmul_mx(
+                out=banks[b][:],
+                lhsT=q_codes[b][:, g * M : (g + 1) * M].bitcast(FP8X4),
+                lhsT_scale=q_scales[b][:, g * M : (g + 1) * M],
+                rhs=kc[:].bitcast(FP8X4),
+                rhs_scale=ks[:],
+                start=(g == 0),
+                stop=(g == G - 1),
+            )
+
+        def place(b):
+            a = ring.tile([M, N], F32, name="a")
+            nc.scalar.copy(a[:], banks[b][:])
+            nc.vector.tensor_copy(placed[b][:].indirect(offs_sb[:, b * (N // 16) : (b + 1) * (N // 16)]), a[:])
+
+        for i in range(len(units) + 2):
+            if i <= last:
+                b, g = units[i]
+                if g == 0:
+                    group_q(b)
+                cast_k(i)
+                if i + LOOKAHEAD <= last:
+                    load_k(i + LOOKAHEAD, 2 if i + LOOKAHEAD == last else 1)
+                    if (i + LOOKAHEAD) % G == 0:
+                        load_q((i + LOOKAHEAD) // G)
+                gather_k(i)
+            if 1 <= i <= last + 1:
+                quantize_k(i - 1)
+                if units[i - 1][1] == 0:
+                    quantize_q(units[i - 1][0])
+                multiply(i - 1)
+            if i >= 2 and units[i - 2][1] == G - 1:
+                place(units[i - 2][0])
+
+        for b in range(B):
+            if b > 0:
+                nc.sync.dma_start(out=out[b, :, : b * SEG], in_=zeros[:, : b * SEG])
+            if b < B - 1:
+                nc.sync.dma_start(out=out[b, :, (b + 1) * SEG :], in_=zeros[:, : T - (b + 1) * SEG])
+        for b in range(B):
+            nc.sync.dma_start(out=out[b, :, b * SEG : (b + 1) * SEG], in_=placed[b][:, b * SEG :])

@@ -28,7 +28,7 @@ LOOKAHEAD = 9
 
 def tile_attend_sddmm_seg_kernel(tc, qT, kT, offs, out):
     nc = tc.nc
-    units = [(b, g) for b in range(B) for g in range(G)]
+    units = [(h, g, u) for h in range(2) for g in range(G) for u in range(2)]
     last = len(units) - 1
 
     with ExitStack() as ctx:
@@ -41,13 +41,11 @@ def tile_attend_sddmm_seg_kernel(tc, qT, kT, offs, out):
         raw_k = {}
         raw_q = {}
 
-        def load_k(i, pieces):
-            b, g = units[i]
+        def load_k(i):
+            h, g, u = units[i]
             rows = kT[g * K_PASS : (g + 1) * K_PASS, :].rearrange("(p t) c -> p t c", t=4)
-            raw = raws.tile([P, 4, SEG], F32, name="raw")
-            step = 4 // pieces
-            for t in range(0, 4, step):
-                nc.sync.dma_start(out=raw[:, t : t + step, :], in_=rows[:, t : t + step, b * SEG : (b + 1) * SEG])
+            raw = raws.tile([P, 2, 2 * SEG], F32, name="raw")
+            nc.sync.dma_start(out=raw[:], in_=rows[:, 2 * u : 2 * u + 2, h * 2 * SEG : (h + 1) * 2 * SEG])
             raw_k[i] = raw
 
         def load_q(b):
@@ -55,27 +53,32 @@ def tile_attend_sddmm_seg_kernel(tc, qT, kT, offs, out):
             nc.sync.dma_start(out=rq[:], in_=qT[b].rearrange("(g p t) m -> p g (t m)", p=P, t=4))
             raw_q[b] = rq
 
-        load_k(0, 2)
-        nc.sync.dma_start(offs_sb[:], offs)
-        load_q(0)
-        for i in range(1, LOOKAHEAD):
-            load_k(i, 1)
-            if i % G == 0:
-                load_q(i // G)
+        q_after = {0: 0, 1: 1, 5: 2, 6: 3}
+
+        def load(i):
+            load_k(i)
+            if i == 0:
+                nc.sync.dma_start(offs_sb[:], offs)
+            if i in q_after:
+                load_q(q_after[i])
+
+        for i in range(LOOKAHEAD):
+            load(i)
 
         zeros = keep.tile([P, T - SEG], F32, name="zeros")
         placed = []
         for b in range(B):
-            row = keep.tile([P, (b + 1) * SEG], F32, name=f"placed{b}")
+            row = keep.tile([P, T], F32, name=f"placed{b}")
             placed.append(row)
         for b in range(B):
-            nc.vector.memset(placed[b][:, b * SEG :], 0.0)
+            nc.vector.memset(placed[b][:, (b // 3) * b * SEG :], 0.0)
         nc.vector.memset(zeros[:], 0.0)
 
-        pairs = []
+        pairs = {}
         for g in range(G):
-            pair = keep.tile([P, 2, T, 2], BF16, name=f"pairs{g}")
-            pairs.append(pair)
+            for u in range(2):
+                pair = keep.tile([P, T, 2], BF16, name=f"pairs{g}{u}")
+                pairs[g, u] = pair
 
         q_codes = []
         q_scales = []
@@ -108,44 +111,44 @@ def tile_attend_sddmm_seg_kernel(tc, qT, kT, offs, out):
                 )
 
         def cast_k(i):
-            b, g = units[i]
-            cols = slice(b * SEG, (b + 1) * SEG)
-            src = raw_k[i][:].rearrange("p (u e) c -> p u c e", e=2)
+            h, g, u = units[i]
+            src = raw_k[i][:].rearrange("p e c -> p c e")
+            dst = pairs[g, u][:, h * 2 * SEG : (h + 1) * 2 * SEG, :]
             if i in (0, last):
-                nc.scalar.activation(pairs[g][:, 0, cols, :], src[:, 0, :, :], COPY)
-                nc.vector.tensor_copy(pairs[g][:, 1, cols, :], src[:, 1, :, :])
+                nc.scalar.activation(dst[:, SEG:, :], src[:, SEG:, :], COPY)
+                nc.vector.tensor_copy(dst[:, :SEG, :], src[:, :SEG, :])
             else:
-                nc.scalar.activation(pairs[g][:, :, cols, :], src, COPY)
+                nc.scalar.activation(dst, src, COPY)
 
         grouped_k = {}
         codes_k = {}
 
         def gather_k(i):
-            b, g = units[i]
-            gk = ring.tile([P, 4 * N], BF16, name="gk", align_bytes=64)
-            words = gk[:].bitcast(U32).rearrange("p (c u) -> p c u", u=2)
-            table = pairs[g][:].rearrange("p u c e -> p (u c e)").bitcast(U32)
-            for u in range(2):
+            h, g, u = units[i]
+            for b in (2 * h, 2 * h + 1):
+                if u == 0:
+                    gk = ring.tile([P, 4 * N], BF16, name="gk", align_bytes=64)
+                    grouped_k[g, b] = gk
+                words = grouped_k[g, b][:].bitcast(U32).rearrange("p (c u) -> p c u", u=2)
+                table = pairs[g, u][:].rearrange("p c e -> p (c e)").bitcast(U32)
                 nc.vector.tensor_copy(
                     words[:, :, u],
-                    table[:, u * T : u * T + (b + 1) * SEG].indirect(offs_sb[:, b * (N // 16) : (b + 1) * (N // 16)]),
+                    table[:, : (b + 1) * SEG].indirect(offs_sb[:, b * (N // 16) : (b + 1) * (N // 16)]),
                 )
-            grouped_k[i] = gk
 
-        def quantize_k(i):
+        def quantize_k(g, b):
             kc = ring.tile([P, N], U32, name="kc", align_bytes=64)
             ks = ring.tile([P, N], U8, name="ks", align_bytes=64)
-            nc.vector.quantize_mx(out=kc[:].bitcast(FP8X4), scales=ks[:], in_=grouped_k[i][:])
-            codes_k[i] = (kc, ks)
+            nc.vector.quantize_mx(out=kc[:].bitcast(FP8X4), scales=ks[:], in_=grouped_k[g, b][:])
+            codes_k[g, b] = (kc, ks)
 
         banks = {}
 
-        def multiply(i):
-            b, g = units[i]
+        def multiply(g, b):
             if g == 0:
                 acc = psum.tile([M, N], F32, name="acc")
                 banks[b] = acc
-            kc, ks = codes_k[i]
+            kc, ks = codes_k[g, b]
             nc.tensor.matmul_mx(
                 out=banks[b][:],
                 lhsT=q_codes[b][:, g * M : (g + 1) * M].bitcast(FP8X4),
@@ -161,29 +164,27 @@ def tile_attend_sddmm_seg_kernel(tc, qT, kT, offs, out):
             nc.scalar.copy(a[:], banks[b][:])
             nc.vector.tensor_copy(placed[b][:].indirect(offs_sb[:, b * (N // 16) : (b + 1) * (N // 16)]), a[:])
 
-        for i in range(len(units) + 2):
+        for i in range(len(units) + 1):
             if i <= last:
-                b, g = units[i]
-                if g == 0:
-                    group_q(b)
                 cast_k(i)
+                if i in q_after:
+                    group_q(q_after[i])
                 if i + LOOKAHEAD <= last:
-                    load_k(i + LOOKAHEAD, 2 if i + LOOKAHEAD == last else 1)
-                    if (i + LOOKAHEAD) % G == 0:
-                        load_q((i + LOOKAHEAD) // G)
+                    load(i + LOOKAHEAD)
                 gather_k(i)
-            if 1 <= i <= last + 1:
-                quantize_k(i - 1)
-                if units[i - 1][1] == 0:
-                    quantize_q(units[i - 1][0])
-                multiply(i - 1)
-            if i >= 2 and units[i - 2][1] == G - 1:
-                place(units[i - 2][0])
+            if i >= 1 and units[i - 1][2] == 1:
+                h, g, u = units[i - 1]
+                for b in (2 * h, 2 * h + 1):
+                    quantize_k(g, b)
+                    if g == 0:
+                        quantize_q(b)
+                    multiply(g, b)
+                if g == G - 1:
+                    for b in (2 * h, 2 * h + 1):
+                        place(b)
 
-        for b in range(B):
-            if b > 0:
-                nc.sync.dma_start(out=out[b, :, : b * SEG], in_=zeros[:, : b * SEG])
-            if b < B - 1:
-                nc.sync.dma_start(out=out[b, :, (b + 1) * SEG :], in_=zeros[:, : T - (b + 1) * SEG])
-        for b in range(B):
-            nc.sync.dma_start(out=out[b, :, b * SEG : (b + 1) * SEG], in_=placed[b][:, b * SEG :])
+        for b in (0, 1):
+            nc.sync.dma_start(out=out[b], in_=placed[b][:])
+        nc.sync.dma_start(out=out[3, :, : 3 * SEG], in_=zeros[:])
+        nc.sync.dma_start(out=out[2], in_=placed[2][:])
+        nc.sync.dma_start(out=out[3, :, 3 * SEG :], in_=placed[3][:, 3 * SEG :])

@@ -7,6 +7,7 @@ FLOPS = 2 * 4 * 128 * 256 * 1536
 F32 = mybir.dt.float32
 BF16 = mybir.dt.bfloat16
 U32 = mybir.dt.uint32
+I32 = mybir.dt.int32
 U16 = mybir.dt.uint16
 U8 = mybir.dt.uint8
 FP8X4 = mybir.dt.float8_e4m3fn_x4
@@ -23,56 +24,30 @@ D = 1536
 M = 128
 K_PASS = 512
 G = D // K_PASS
-LOOKAHEAD = 9
+
+UNITS = [(h, g, u) for h in range(2) for g in range(G) for u in range(2)]
+SPLIT = {0: 2}
+PLAN = {0: (("V", 0, 512), ("S", 512, 1024))}
+LOADS = [("k", i) for i in range(6)] + [("q", 0), ("q", 1)] + [("k", i) for i in range(6, 12)] + [("q", 2), ("q", 3)]
+Q_ENGINES = ("GGG", "GGG", "SGG", "SSG")
+AHEAD = 11
+RAW_BUFS = 9
 
 
 def tile_attend_sddmm_seg_kernel(tc, qT, kT, offs, out):
     nc = tc.nc
-    units = [(h, g, u) for h in range(2) for g in range(G) for u in range(2)]
-    last = len(units) - 1
 
     with ExitStack() as ctx:
         keep = ctx.enter_context(tc.tile_pool(name="keep", bufs=1))
-        raws = ctx.enter_context(tc.tile_pool(name="raws", bufs=LOOKAHEAD + 1))
-        ring = ctx.enter_context(tc.tile_pool(name="ring", bufs=4))
+        raws = ctx.enter_context(tc.tile_pool(name="raws", bufs=RAW_BUFS))
+        ring = ctx.enter_context(tc.tile_pool(name="ring", bufs=2))
+        qpool = ctx.enter_context(tc.tile_pool(name="qpool", bufs=2))
         psum = ctx.enter_context(tc.psum_pool(name="psum", bufs=B))
 
         offs_sb = keep.tile([P, B * N // 16], U16, name="offs_sb")
-        raw_k = {}
-        raw_q = {}
 
-        def load_k(i):
-            h, g, u = units[i]
-            rows = kT[g * K_PASS : (g + 1) * K_PASS, :].rearrange("(p t) c -> p t c", t=4)
-            raw = raws.tile([P, 2, 2 * SEG], F32, name="raw")
-            nc.sync.dma_start(out=raw[:], in_=rows[:, 2 * u : 2 * u + 2, h * 2 * SEG : (h + 1) * 2 * SEG])
-            raw_k[i] = raw
-
-        def load_q(b):
-            rq = keep.tile([P, G, 4 * M], F32, name=f"raw_q{b}")
-            nc.sync.dma_start(out=rq[:], in_=qT[b].rearrange("(g p t) m -> p g (t m)", p=P, t=4))
-            raw_q[b] = rq
-
-        q_after = {0: 0, 1: 1, 5: 2, 6: 3}
-
-        def load(i):
-            load_k(i)
-            if i == 0:
-                nc.sync.dma_start(offs_sb[:], offs)
-            if i in q_after:
-                load_q(q_after[i])
-
-        for i in range(LOOKAHEAD):
-            load(i)
-
-        zeros = keep.tile([P, T - SEG], F32, name="zeros")
-        placed = []
-        for b in range(B):
-            row = keep.tile([P, T], F32, name=f"placed{b}")
-            placed.append(row)
-        for b in range(B):
-            nc.vector.memset(placed[b][:, (b // 3) * b * SEG :], 0.0)
-        nc.vector.memset(zeros[:], 0.0)
+        def token_list(b):
+            return offs_sb[:, b * (N // 16) : (b + 1) * (N // 16)]
 
         pairs = {}
         for g in range(G):
@@ -80,111 +55,199 @@ def tile_attend_sddmm_seg_kernel(tc, qT, kT, offs, out):
                 pair = keep.tile([P, T, 2], BF16, name=f"pairs{g}{u}")
                 pairs[g, u] = pair
 
-        q_codes = []
-        q_scales = []
-        for b in range(B):
-            qc = keep.tile([P, G * M], U32, name=f"q_codes{b}", align_bytes=64)
-            qs = keep.tile([P, G * M], U8, name=f"q_scales{b}", align_bytes=64)
-            q_codes.append(qc)
-            q_scales.append(qs)
+        raw_k = {}
+        raw_q = {}
 
-        grouped_q = {}
-
-        def group_q(b):
-            gq = keep.tile([P, G * M * 4], BF16, name=f"grouped_q{b}", align_bytes=64)
-            nc.gpsimd.tensor_scalar(
-                out=gq[:].rearrange("p (g m t) -> p g m t", g=G, t=4),
-                in0=raw_q[b][:].rearrange("p g (t m) -> p g m t", t=4),
-                scalar1=1.0,
-                scalar2=0.0,
-                op0=MULT,
-                op1=ADD,
-            )
-            grouped_q[b] = gq
-
-        def quantize_q(b):
-            for lo, hi in ((0, 256), (256, 384)):
-                nc.vector.quantize_mx(
-                    out=q_codes[b][:, lo:hi].bitcast(FP8X4),
-                    scales=q_scales[b][:, lo:hi],
-                    in_=grouped_q[b][:, 4 * lo : 4 * hi],
+        def load_k(i):
+            h, g, u = UNITS[i]
+            rows = kT[g * K_PASS : (g + 1) * K_PASS, :].rearrange("(p t) c -> p t c", t=4)
+            raw = raws.tile([P, 2, 2 * SEG], F32, name="raw")
+            parts = SPLIT.get(i, 1)
+            width = 2 * SEG // parts
+            for j in range(parts):
+                lo = h * 2 * SEG + j * width
+                nc.sync.dma_start(
+                    out=raw[:, :, j * width : (j + 1) * width],
+                    in_=rows[:, 2 * u : 2 * u + 2, lo : lo + width],
                 )
+                if i == 0 and j == 0:
+                    nc.sync.dma_start(offs_sb[:], offs)
+            raw_k[i] = raw
 
-        def cast_k(i):
-            h, g, u = units[i]
-            src = raw_k[i][:].rearrange("p e c -> p c e")
-            dst = pairs[g, u][:, h * 2 * SEG : (h + 1) * 2 * SEG, :]
-            if i in (0, last):
-                nc.scalar.activation(dst[:, SEG:, :], src[:, SEG:, :], COPY)
-                nc.vector.tensor_copy(dst[:, :SEG, :], src[:, :SEG, :])
+        def load_q(b):
+            rq = qpool.tile([P, G, 4 * M], F32, name="rq")
+            nc.sync.dma_start(out=rq[:], in_=qT[b].rearrange("(g p t) m -> p g (t m)", p=P, t=4))
+            raw_q[b] = rq
+
+        loads = list(LOADS)
+
+        def load_next(count):
+            for n in range(min(count, len(loads))):
+                kind, x = loads.pop(0)
+                if kind == "k":
+                    load_k(x)
+                else:
+                    load_q(x)
+
+        zeros = keep.tile([P, 2 * SEG], F32, name="zeros")
+        placed = []
+
+        def fill():
+            for b in range(B):
+                row = keep.tile([P, (b // 2 + 1) * 2 * SEG], F32, name=f"placed{b}")
+                placed.append(row)
+                nc.gpsimd.memset(row[:, (0, 0, 2, 3)[b] * SEG :], 0.0)
+            nc.gpsimd.memset(zeros[:], 0.0)
+
+        def cast(i, engine, lo, hi):
+            h, g, u = UNITS[i]
+            src = raw_k[i][:].rearrange("p e c -> p c e")[:, lo:hi, :]
+            dst = pairs[g, u][:, h * 2 * SEG + lo : h * 2 * SEG + hi, :]
+            if engine == "V":
+                nc.vector.tensor_copy(dst, src)
             else:
                 nc.scalar.activation(dst, src, COPY)
 
+        picked_k = {}
         grouped_k = {}
         codes_k = {}
 
-        def gather_k(i):
-            h, g, u = units[i]
-            for b in (2 * h, 2 * h + 1):
-                if u == 0:
-                    gk = ring.tile([P, 4 * N], BF16, name="gk", align_bytes=64)
-                    grouped_k[g, b] = gk
-                words = grouped_k[g, b][:].bitcast(U32).rearrange("p (c u) -> p c u", u=2)
-                table = pairs[g, u][:].rearrange("p c e -> p (c e)").bitcast(U32)
-                nc.vector.tensor_copy(
-                    words[:, :, u],
-                    table[:, : (b + 1) * SEG].indirect(offs_sb[:, b * (N // 16) : (b + 1) * (N // 16)]),
-                )
+        def gather(g, u, b):
+            table = pairs[g, u][:].rearrange("p c e -> p (c e)").bitcast(U32)[:, : (b + 1) * SEG]
+            h = b // 2
+            if (h, g) not in grouped_k:
+                gk = ring.tile([P, 2, N * 4], BF16, name="gk", align_bytes=64)
+                grouped_k[h, g] = gk
+            words = grouped_k[h, g][:, b % 2, :].bitcast(U32).rearrange("p (c u) -> p c u", u=2)
+            nc.vector.tensor_copy(words[:, :, u], table.indirect(token_list(b)))
 
-        def quantize_k(g, b):
-            kc = ring.tile([P, N], U32, name="kc", align_bytes=64)
-            ks = ring.tile([P, N], U8, name="ks", align_bytes=64)
-            nc.vector.quantize_mx(out=kc[:].bitcast(FP8X4), scales=ks[:], in_=grouped_k[g, b][:])
-            codes_k[g, b] = (kc, ks)
+        def interleave(h, g):
+            return
+
+        def quantize_k(h, g):
+            kc = keep.tile([P, 2 * N], U32, name=f"kc{h}{g}", align_bytes=64)
+            ks = keep.tile([P, 2 * N], U8, name=f"ks{h}{g}", align_bytes=64)
+            nc.vector.quantize_mx(
+                out=kc[:].bitcast(FP8X4), scales=ks[:], in_=grouped_k[h, g][:].rearrange("p b x -> p (b x)")
+            )
+            codes_k[h, g] = (kc, ks)
+
+        grouped_q = {}
+        codes_q = {}
+
+        def group_q(b):
+            gq = keep.tile([P, G * M * 4], BF16, name=f"grouped_q{b}", align_bytes=64)
+            dst = gq[:].rearrange("p (g m t) -> p g m t", g=G, t=4)
+            src = raw_q[b][:].rearrange("p g (t m) -> p g m t", t=4)
+            for g in range(G):
+                if Q_ENGINES[b][g] == "S":
+                    nc.scalar.activation(dst[:, g], src[:, g], COPY)
+                elif Q_ENGINES[b][g] == "V":
+                    nc.vector.tensor_copy(dst[:, g], src[:, g])
+                else:
+                    nc.gpsimd.tensor_scalar(out=dst[:, g], in0=src[:, g], scalar1=1.0, scalar2=0.0, op0=MULT, op1=ADD)
+            grouped_q[b] = gq
+
+        def quantize_q(b):
+            qc = keep.tile([P, G * M], U32, name=f"q_codes{b}", align_bytes=64)
+            qs = keep.tile([P, G * M], U8, name=f"q_scales{b}", align_bytes=64)
+            for lo, hi in ((0, 256), (256, 384)):
+                nc.vector.quantize_mx(
+                    out=qc[:, lo:hi].bitcast(FP8X4), scales=qs[:, lo:hi], in_=grouped_q[b][:, 4 * lo : 4 * hi]
+                )
+            codes_q[b] = (qc, qs)
 
         banks = {}
 
-        def multiply(g, b):
-            if g == 0:
-                acc = psum.tile([M, N], F32, name="acc")
-                banks[b] = acc
-            kc, ks = codes_k[g, b]
-            nc.tensor.matmul_mx(
-                out=banks[b][:],
-                lhsT=q_codes[b][:, g * M : (g + 1) * M].bitcast(FP8X4),
-                lhsT_scale=q_scales[b][:, g * M : (g + 1) * M],
-                rhs=kc[:].bitcast(FP8X4),
-                rhs_scale=ks[:],
-                start=(g == 0),
-                stop=(g == G - 1),
-            )
+        def multiply(b):
+            acc = psum.tile([M, N], F32, name="acc")
+            qc, qs = codes_q[b]
+            cols = slice((b % 2) * N, (b % 2 + 1) * N)
+            for g in range(G):
+                kc, ks = codes_k[b // 2, g]
+                nc.tensor.matmul_mx(
+                    out=acc[:],
+                    lhsT=qc[:, g * M : (g + 1) * M].bitcast(FP8X4),
+                    lhsT_scale=qs[:, g * M : (g + 1) * M],
+                    rhs=kc[:, cols].bitcast(FP8X4),
+                    rhs_scale=ks[:, cols],
+                    start=(g == 0),
+                    stop=(g == G - 1),
+                )
+            banks[b] = acc
 
-        def place(b):
-            a = ring.tile([M, N], F32, name="a")
-            nc.scalar.copy(a[:], banks[b][:])
-            nc.vector.tensor_copy(placed[b][:].indirect(offs_sb[:, b * (N // 16) : (b + 1) * (N // 16)]), a[:])
+        scores = {}
 
-        for i in range(len(units) + 1):
-            if i <= last:
-                cast_k(i)
-                if i in q_after:
-                    group_q(q_after[i])
-                if i + LOOKAHEAD <= last:
-                    load(i + LOOKAHEAD)
-                gather_k(i)
-            if i >= 1 and units[i - 1][2] == 1:
-                h, g, u = units[i - 1]
-                for b in (2 * h, 2 * h + 1):
-                    quantize_k(g, b)
-                    if g == 0:
-                        quantize_q(b)
-                    multiply(g, b)
-                if g == G - 1:
-                    for b in (2 * h, 2 * h + 1):
-                        place(b)
+        def empty(b, engine):
+            a = keep.tile([M, N], F32, name=f"a{b}")
+            if engine == "V":
+                nc.vector.tensor_copy(a[:], banks[b][:])
+            else:
+                nc.scalar.copy(a[:], banks[b][:])
+            scores[b] = a
 
-        for b in (0, 1):
-            nc.sync.dma_start(out=out[b], in_=placed[b][:])
-        nc.sync.dma_start(out=out[3, :, : 3 * SEG], in_=zeros[:])
-        nc.sync.dma_start(out=out[2], in_=placed[2][:])
-        nc.sync.dma_start(out=out[3, :, 3 * SEG :], in_=placed[3][:, 3 * SEG :])
+        def scatter(b):
+            nc.vector.tensor_copy(placed[b][:].indirect(token_list(b)), scores[b][:])
+
+        load_next(AHEAD)
+        fill()
+
+        late = []
+        for i in range(len(UNITS)):
+            h, g, u = UNITS[i]
+            if i == 6:
+                for f, x in late:
+                    f(*x)
+                late = []
+                group_q(0)
+                group_q(1)
+                load_next(2)
+                quantize_q(0)
+                multiply(0)
+                empty(0, "S")
+                quantize_q(1)
+                multiply(1)
+                scatter(0)
+                empty(1, "V")
+                scatter(1)
+            plan = PLAN.get(i, (("S", 0, 2 * SEG),))
+            b0 = 2 * h
+            done = set()
+            for engine, lo, hi in plan:
+                cast(i, engine, lo, hi)
+                if hi == SEG:
+                    gather(g, u, b0)
+                    done.add(b0)
+            load_next(1)
+            if b0 not in done:
+                gather(g, u, b0)
+            for f, x in late[:1]:
+                f(*x)
+            late = late[1:]
+            gather(g, u, b0 + 1)
+            for f, x in late:
+                f(*x)
+            late = []
+            if u == 1:
+                late = [(interleave, (h, g)), (quantize_k, (h, g))]
+        for f, x in late:
+            f(*x)
+        group_q(2)
+        group_q(3)
+        quantize_q(2)
+        multiply(2)
+        empty(2, "S")
+        quantize_q(3)
+        multiply(3)
+        empty(3, "S")
+        scatter(2)
+        scatter(3)
+
+
+        for b in range(B):
+            start = (1 - b // 2) * 2 * SEG
+            nc.sync.dma_start(out=out[b, :, start : start + 2 * SEG], in_=zeros[:])
+        nc.sync.dma_start(out=out[3, :, 2 * SEG : 3 * SEG], in_=zeros[:, :SEG])
+        for b in range(B):
+            start, stop = ((0, 2), (0, 2), (2, 4), (3, 4))[b]
+            nc.sync.dma_start(out=out[b, :, start * SEG : stop * SEG], in_=placed[b][:, start * SEG : stop * SEG])

@@ -26,10 +26,10 @@ K_PASS = 512
 G = D // K_PASS
 
 UNITS = [(h, g, u) for h in range(2) for g in range(G) for u in range(2)]
-SPLIT = {0: 2}
+SPLIT = {}
 PLAN = {0: (("V", 0, 512), ("S", 512, 1024))}
 LOADS = [("k", i) for i in range(6)] + [("q", 0), ("q", 1)] + [("k", i) for i in range(6, 12)] + [("q", 2), ("q", 3)]
-Q_ENGINES = ("GGG", "GGG", "SGG", "SSG")
+Q_PLAN = ((("S",0,3),),(("S",0,3),),(("S",0,3),),(("S",0,3),))
 AHEAD = 11
 RAW_BUFS = 9
 
@@ -96,8 +96,8 @@ def tile_attend_sddmm_seg_kernel(tc, qT, kT, offs, out):
             for b in range(B):
                 row = keep.tile([P, (b // 2 + 1) * 2 * SEG], F32, name=f"placed{b}")
                 placed.append(row)
-                nc.gpsimd.memset(row[:, (0, 0, 2, 3)[b] * SEG :], 0.0)
-            nc.gpsimd.memset(zeros[:], 0.0)
+                nc.vector.memset(row[:, (0, 0, 2, 3)[b] * SEG :], 0.0)
+            nc.vector.memset(zeros[:], 0.0)
 
         def cast(i, engine, lo, hi):
             h, g, u = UNITS[i]
@@ -139,13 +139,13 @@ def tile_attend_sddmm_seg_kernel(tc, qT, kT, offs, out):
             gq = keep.tile([P, G * M * 4], BF16, name=f"grouped_q{b}", align_bytes=64)
             dst = gq[:].rearrange("p (g m t) -> p g m t", g=G, t=4)
             src = raw_q[b][:].rearrange("p g (t m) -> p g m t", t=4)
-            for g in range(G):
-                if Q_ENGINES[b][g] == "S":
-                    nc.scalar.activation(dst[:, g], src[:, g], COPY)
-                elif Q_ENGINES[b][g] == "V":
-                    nc.vector.tensor_copy(dst[:, g], src[:, g])
+            for engine, lo, hi in Q_PLAN[b]:
+                if engine == "S":
+                    nc.scalar.activation(dst[:, lo:hi], src[:, lo:hi], COPY)
+                elif engine == "V":
+                    nc.vector.tensor_copy(dst[:, lo:hi], src[:, lo:hi])
                 else:
-                    nc.gpsimd.tensor_scalar(out=dst[:, g], in0=src[:, g], scalar1=1.0, scalar2=0.0, op0=MULT, op1=ADD)
+                    nc.gpsimd.tensor_scalar(out=dst[:, lo:hi], in0=src[:, lo:hi], scalar1=1.0, scalar2=0.0, op0=MULT, op1=ADD)
             grouped_q[b] = gq
 
         def quantize_q(b):

@@ -94,10 +94,10 @@ def tile_attend_sddmm_seg_kernel(tc, qT, kT, offs, out):
 
         def fill():
             for b in range(B):
-                row = keep.tile([P, (b // 2 + 1) * 2 * SEG], F32, name=f"placed{b}")
+                row = keep.tile([P, T], F32, name=f"placed{b}")
                 placed.append(row)
-                nc.vector.memset(row[:, (0, 0, 2, 3)[b] * SEG :], 0.0)
-            nc.vector.memset(zeros[:], 0.0)
+                nc.gpsimd.memset(row[:, (0, 0, 2, 3)[b] * SEG :], 0.0)
+            nc.gpsimd.memset(zeros[:], 0.0)
 
         def cast(i, engine, lo, hi):
             h, g, u = UNITS[i]
@@ -115,14 +115,18 @@ def tile_attend_sddmm_seg_kernel(tc, qT, kT, offs, out):
         def gather(g, u, b):
             table = pairs[g, u][:].rearrange("p c e -> p (c e)").bitcast(U32)[:, : (b + 1) * SEG]
             h = b // 2
-            if (h, g) not in grouped_k:
-                gk = ring.tile([P, 2, N * 4], BF16, name="gk", align_bytes=64)
-                grouped_k[h, g] = gk
-            words = grouped_k[h, g][:, b % 2, :].bitcast(U32).rearrange("p (c u) -> p c u", u=2)
-            nc.vector.tensor_copy(words[:, :, u], table.indirect(token_list(b)))
+            if (h, g) not in picked_k:
+                picked = ring.tile([P, 2, 2, N], U32, name="picked")
+                picked_k[h, g] = picked
+            nc.vector.tensor_copy(picked_k[h, g][:, b % 2, u, :], table.indirect(token_list(b)))
 
         def interleave(h, g):
-            return
+            gk = ring.tile([P, 2, N * 4], BF16, name="gk", align_bytes=64)
+            nc.vector.tensor_copy(
+                gk[:].rearrange("p b x -> p (b x)").bitcast(I32).rearrange("p (b c u) -> p b c u", b=2, u=2),
+                picked_k[h, g][:].rearrange("p b u c -> p (b u c)").bitcast(I32).rearrange("p (b u c) -> p b c u", b=2, u=2),
+            )
+            grouped_k[h, g] = gk
 
         def quantize_k(h, g):
             kc = keep.tile([P, 2 * N], U32, name=f"kc{h}{g}", align_bytes=64)
@@ -221,15 +225,13 @@ def tile_attend_sddmm_seg_kernel(tc, qT, kT, offs, out):
             load_next(1)
             if b0 not in done:
                 gather(g, u, b0)
-            for f, x in late[:1]:
-                f(*x)
-            late = late[1:]
-            gather(g, u, b0 + 1)
             for f, x in late:
                 f(*x)
             late = []
+            gather(g, u, b0 + 1)
             if u == 1:
-                late = [(interleave, (h, g)), (quantize_k, (h, g))]
+                interleave(h, g)
+                late = [(quantize_k, (h, g))]
         for f, x in late:
             f(*x)
         group_q(2)
@@ -244,10 +246,10 @@ def tile_attend_sddmm_seg_kernel(tc, qT, kT, offs, out):
         scatter(3)
 
 
-        for b in range(B):
-            start = (1 - b // 2) * 2 * SEG
-            nc.sync.dma_start(out=out[b, :, start : start + 2 * SEG], in_=zeros[:])
+        for b in (0, 1):
+            nc.sync.dma_start(out=out[b], in_=placed[b][:])
+        for b in (2, 3):
+            nc.sync.dma_start(out=out[b, :, : 2 * SEG], in_=zeros[:])
         nc.sync.dma_start(out=out[3, :, 2 * SEG : 3 * SEG], in_=zeros[:, :SEG])
-        for b in range(B):
-            start, stop = ((0, 2), (0, 2), (2, 4), (3, 4))[b]
-            nc.sync.dma_start(out=out[b, :, start * SEG : stop * SEG], in_=placed[b][:, start * SEG : stop * SEG])
+        nc.sync.dma_start(out=out[2, :, 2 * SEG :], in_=placed[2][:, 2 * SEG :])
+        nc.sync.dma_start(out=out[3, :, 3 * SEG :], in_=placed[3][:, 3 * SEG :])

from contextlib import ExitStack

import concourse.mybir as mybir

FLOPS = 2 * 4 * 128 * 256 * 1536

F32 = mybir.dt.float32
BF16 = mybir.dt.bfloat16
U32 = mybir.dt.uint32
I32 = mybir.dt.int32
U16 = mybir.dt.uint16
U8 = mybir.dt.uint8
FP8X4 = mybir.dt.float8_e4m3fn_x4
COPY = mybir.ActivationFunctionType.Copy
MULT = mybir.AluOpType.mult
ADD = mybir.AluOpType.add

P = 128
B = 4
N = 256
T = 2048
SEG = T // B
D = 1536
M = 128
K_PASS = 512
G = D // K_PASS

UNITS = [(h, g, u) for h in range(2) for g in range(G) for u in range(2)]
SPLIT = {}
PLAN = {0: (("V", 0, 512), ("S", 512, 1024))}
LOADS = [("k", i) for i in range(6)] + [("q", 0), ("q", 1)] + [("k", i) for i in range(6, 12)] + [("q", 2), ("q", 3)]
Q_PLAN = ((("S",0,3),),(("S",0,3),),(("S",0,3),),(("S",0,3),))
AHEAD = 11
RAW_BUFS = 9


def tile_attend_sddmm_seg_kernel(tc, qT, kT, offs, out):
    nc = tc.nc

    with ExitStack() as ctx:
        keep = ctx.enter_context(tc.tile_pool(name="keep", bufs=1))
        raws = ctx.enter_context(tc.tile_pool(name="raws", bufs=RAW_BUFS))
        ring = ctx.enter_context(tc.tile_pool(name="ring", bufs=2))
        qpool = ctx.enter_context(tc.tile_pool(name="qpool", bufs=2))
        psum = ctx.enter_context(tc.psum_pool(name="psum", bufs=B))

        offs_sb = keep.tile([P, B * N // 16], U16, name="offs_sb")

        def token_list(b):
            return offs_sb[:, b * (N // 16) : (b + 1) * (N // 16)]

        pairs = {}
        for g in range(G):
            for u in range(2):
                pair = keep.tile([P, T, 2], BF16, name=f"pairs{g}{u}")
                pairs[g, u] = pair

        raw_k = {}
        raw_q = {}

        def load_k(i):
            h, g, u = UNITS[i]
            rows = kT[g * K_PASS : (g + 1) * K_PASS, :].rearrange("(p t) c -> p t c", t=4)
            raw = raws.tile([P, 2, 2 * SEG], F32, name="raw")
            parts = SPLIT.get(i, 1)
            width = 2 * SEG // parts
            for j in range(parts):
                lo = h * 2 * SEG + j * width
                nc.sync.dma_start(
                    out=raw[:, :, j * width : (j + 1) * width],
                    in_=rows[:, 2 * u : 2 * u + 2, lo : lo + width],
                )
                if i == 0 and j == 0:
                    nc.sync.dma_start(offs_sb[:], offs)
            raw_k[i] = raw

        def load_q(b):
            rq = qpool.tile([P, G, 4 * M], F32, name="rq")
            nc.sync.dma_start(out=rq[:], in_=qT[b].rearrange("(g p t) m -> p g (t m)", p=P, t=4))
            raw_q[b] = rq

        loads = list(LOADS)

        def load_next(count):
            for n in range(min(count, len(loads))):
                kind, x = loads.pop(0)
                if kind == "k":
                    load_k(x)
                else:
                    load_q(x)

        zeros = keep.tile([P, 2 * SEG], F32, name="zeros")
        placed = []

        def fill():
            for b in range(B):
                row = keep.tile([P, T], F32, name=f"placed{b}")
                placed.append(row)
                nc.gpsimd.memset(row[:, (0, 0, 2, 3)[b] * SEG :], 0.0)
            nc.gpsimd.memset(zeros[:], 0.0)

        def cast(i, engine, lo, hi):
            h, g, u = UNITS[i]
            src = raw_k[i][:].rearrange("p e c -> p c e")[:, lo:hi, :]
            dst = pairs[g, u][:, h * 2 * SEG + lo : h * 2 * SEG + hi, :]
            if engine == "V":
                nc.vector.tensor_copy(dst, src)
            else:
                nc.scalar.activation(dst, src, COPY)

        picked_k = {}
        grouped_k = {}
        codes_k = {}

        def gather(g, u, b):
            table = pairs[g, u][:].rearrange("p c e -> p (c e)").bitcast(U32)[:, : (b + 1) * SEG]
            h = b // 2
            if (h, g) not in picked_k:
                picked = ring.tile([P, 2, 2, N], U32, name="picked")
                picked_k[h, g] = picked
            nc.vector.tensor_copy(picked_k[h, g][:, b % 2, u, :], table.indirect(token_list(b)))

        def interleave(h, g):
            gk = ring.tile([P, 2, N * 4], BF16, name="gk", align_bytes=64)
            nc.vector.tensor_copy(
                gk[:].rearrange("p b x -> p (b x)").bitcast(I32).rearrange("p (b c u) -> p b c u", b=2, u=2),
                picked_k[h, g][:].rearrange("p b u c -> p (b u c)").bitcast(I32).rearrange("p (b u c) -> p b c u", b=2, u=2),
            )
            grouped_k[h, g] = gk

        def quantize_k(h, g):
            kc = keep.tile([P, 2 * N], U32, name=f"kc{h}{g}", align_bytes=64)
            ks = keep.tile([P, 2 * N], U8, name=f"ks{h}{g}", align_bytes=64)
            nc.vector.quantize_mx(
                out=kc[:].bitcast(FP8X4), scales=ks[:], in_=grouped_k[h, g][:].rearrange("p b x -> p (b x)")
            )
            codes_k[h, g] = (kc, ks)

        grouped_q = {}
        codes_q = {}

        def group_q(b):
            gq = keep.tile([P, G * M * 4], BF16, name=f"grouped_q{b}", align_bytes=64)
            dst = gq[:].rearrange("p (g m t) -> p g m t", g=G, t=4)
            src = raw_q[b][:].rearrange("p g (t m) -> p g m t", t=4)
            for engine, lo, hi in Q_PLAN[b]:
                if engine == "S":
                    nc.scalar.activation(dst[:, lo:hi], src[:, lo:hi], COPY)
                elif engine == "V":
                    nc.vector.tensor_copy(dst[:, lo:hi], src[:, lo:hi])
                else:
                    nc.gpsimd.tensor_scalar(out=dst[:, lo:hi], in0=src[:, lo:hi], scalar1=1.0, scalar2=0.0, op0=MULT, op1=ADD)
            grouped_q[b] = gq

        def quantize_q(b):
            qc = keep.tile([P, G * M], U32, name=f"q_codes{b}", align_bytes=64)
            qs = keep.tile([P, G * M], U8, name=f"q_scales{b}", align_bytes=64)
            for lo, hi in ((0, 256), (256, 384)):
                nc.vector.quantize_mx(
                    out=qc[:, lo:hi].bitcast(FP8X4), scales=qs[:, lo:hi], in_=grouped_q[b][:, 4 * lo : 4 * hi]
                )
            codes_q[b] = (qc, qs)

        banks = {}

        def multiply(b):
            acc = psum.tile([M, N], F32, name="acc")
            qc, qs = codes_q[b]
            cols = slice((b % 2) * N, (b % 2 + 1) * N)
            for g in range(G):
                kc, ks = codes_k[b // 2, g]
                nc.tensor.matmul_mx(
                    out=acc[:],
                    lhsT=qc[:, g * M : (g + 1) * M].bitcast(FP8X4),
                    lhsT_scale=qs[:, g * M : (g + 1) * M],
                    rhs=kc[:, cols].bitcast(FP8X4),
                    rhs_scale=ks[:, cols],
                    start=(g == 0),
                    stop=(g == G - 1),
                )
            banks[b] = acc

        scores = {}

        def empty(b, engine):
            a = keep.tile([M, N], F32, name=f"a{b}")
            if engine == "V":
                nc.vector.tensor_copy(a[:], banks[b][:])
            else:
                nc.scalar.copy(a[:], banks[b][:])
            scores[b] = a

        def scatter(b):
            nc.vector.tensor_copy(placed[b][:].indirect(token_list(b)), scores[b][:])

        load_next(AHEAD)
        fill()

        late = []
        for i in range(len(UNITS)):
            h, g, u = UNITS[i]
            if i == 6:
                for f, x in late:
                    f(*x)
                late = []
                group_q(0)
                group_q(1)
                load_next(2)
                quantize_q(0)
                multiply(0)
                empty(0, "S")
                quantize_q(1)
                multiply(1)
                scatter(0)
                empty(1, "V")
                scatter(1)
            plan = PLAN.get(i, (("S", 0, 2 * SEG),))
            b0 = 2 * h
            done = set()
            for engine, lo, hi in plan:
                cast(i, engine, lo, hi)
                if hi == SEG:
                    gather(g, u, b0)
                    done.add(b0)
            load_next(1)
            if b0 not in done:
                gather(g, u, b0)
            for f, x in late:
                f(*x)
            late = []
            gather(g, u, b0 + 1)
            if u == 1:
                interleave(h, g)
                late = [(quantize_k, (h, g))]
        for f, x in late:
            f(*x)
        group_q(2)
        group_q(3)
        quantize_q(2)
        multiply(2)
        empty(2, "S")
        quantize_q(3)
        multiply(3)
        empty(3, "S")
        scatter(2)
        scatter(3)


        for b in (0, 1):
            nc.sync.dma_start(out=out[b], in_=placed[b][:])
        for b in (2, 3):
            nc.sync.dma_start(out=out[b, :, : 2 * SEG], in_=zeros[:])
        nc.sync.dma_start(out=out[3, :, 2 * SEG : 3 * SEG], in_=zeros[:, :SEG])
        nc.sync.dma_start(out=out[2, :, 2 * SEG :], in_=placed[2][:, 2 * SEG :])
        nc.sync.dma_start(out=out[3, :, 3 * SEG :], in_=placed[3][:, 3 * SEG :])
